import numpy as np
CORES = [144,145,146,147,148,149,150,151,272,273,274,275,276,277,278,279]
N = 16
def setup_inputs(rng):
    return {"x1": rng.standard_normal((N, 128, 16), dtype=np.float32), "x2": rng.standard_normal((N, 128, 512), dtype=np.float32)}
def reference(x1, x2):
    out = []
    b = 16 // N
    bl = x1.reshape(N, 128, N, b)
    out.append(np.ascontiguousarray(bl.transpose(2, 1, 0, 3)).reshape(N, 128, 16))
    out.append(np.broadcast_to(x2[8], x2.shape))
    return {"y1": out[0], "y2": out[1]}

@@ -1,0 +1,158 @@
+from concourse.bass import DstId, RemoteDMATransfer
+
+WAVES = 1
+SPLIT = True
+ROOT_CARRIES = False
+DUP_A = False
+
+PIECES = 16
+SCRATCH = {
+    "s1": ("sbuf", [128, 16], "float32"),
+    "land": ("sbuf", [128, 16], "float32"),
+    "d": ("dram", [PIECES, 128, 32], "float32"),
+}
+SEMAPHORES = ["ld1", "arr1", "st1", "sent", "go", "st2"] + [n + str(w) for w in range(WAVES) for n in ("ld2", "own", "arr2")]
+
+
+def bits(lo, n):
+    return ((1 << n) - 1) << lo
+
+
+def pop(mask):
+    return bin(mask).count("1")
+
+
+def a2a_calls(r):
+    near = [j for j in range(16) if j // 8 == r // 8 and j != r]
+    far = [j for j in range(16) if j // 8 != r // 8]
+    on = [(j, bits(8 + i, 1)) for i, j in enumerate(near)]
+    if SPLIT and r > 8 and not ROOT_CARRIES:
+        return [on + [(j, bits(2 * i, 2)) for i, j in enumerate(far[:4])],
+                [(j, bits(2 * i, 2)) for i, j in enumerate(far[4:])]]
+    return [on + [(j, bits(i, 1)) for i, j in enumerate(far)]]
+
+
+def wave(w):
+    n = PIECES // WAVES
+    return list(range(w * n, (w + 1) * n))
+
+
+def carrier(i):
+    return 1 if i % 8 < 2 else i % 8
+
+
+def a_owners(i):
+    return [i % 4, 4 + i % 4] if DUP_A else [i % 8]
+
+
+def bcast_calls(rank, w):
+    own, arr = "own%d" % w, "arr2%d" % w
+    if rank == 8:
+        ps = wave(w)
+        if ROOT_CARRIES:
+            calls = []
+            for c in range(0, len(ps), 8):
+                part = ps[c:c + 8]
+                calls.append([(i, a_owners(i), bits(t, 1), own) for t, i in enumerate(part)]
+                             + [(i, [8 + carrier(i)], bits(8 + t, 1), own) for t, i in enumerate(part)])
+            return calls
+        e = 16 // len(ps)
+        return [[(i, [8 + carrier(i)], bits(t * e, e), own) for t, i in enumerate(ps)]]
+    if rank > 8:
+        ps = [i for i in wave(w) if carrier(i) == rank - 8]
+        others = [j for j in range(9, 16) if j != rank]
+        if ROOT_CARRIES:
+            e = 16 // len(ps)
+            return [[(i, others, bits(t * e, e), arr) for t, i in enumerate(ps)]]
+        e = 8 // len(ps)
+        return [[(i, a_owners(i), bits(t * e, e), own) for t, i in enumerate(ps)]
+                + [(i, others, bits(8 + t * e, e), arr) for t, i in enumerate(ps)]]
+    ps = [i for i in wave(w) if rank in a_owners(i)]
+    e = 16 // len(ps)
+    mates = [j for j in range(8) if j != rank and (j // 4 == rank // 4 or not DUP_A)]
+    return [[(i, mates, bits(t * e, e), arr) for t, i in enumerate(ps)]]
+
+
+def expect(rank):
+    n = {}
+    for s in range(16):
+        for call in a2a_calls(s):
+            for j, mask in call:
+                if j == rank:
+                    n["arr1"] = n.get("arr1", 0) + pop(mask)
+        for w in range(WAVES):
+            for call in bcast_calls(s, w):
+                for tr in call:
+                    if rank in tr[1]:
+                        n[tr[3]] = n.get(tr[3], 0) + pop(tr[2])
+    return n
+
+
+def rank_program(g, core, T, topo):
+    rank = T.rank_of(core)
+    if rank is None:
+        return
+    sem = T.sem
+    exp = expect(rank)
+    sent = [0]
+
+    def dst_id(j):
+        rid, pid = topo.addr(T.cores[j], core)
+        return DstId(rid=rid, pnc=pid)
+
+    def a2a(call):
+        g.remote_dma_fused(
+            [RemoteDMATransfer(dst_ids=[dst_id(j)], dma_engine_mask=mask, remote_sem=sem.arr1,
+                               srcs=[T.s1[:, j:j + 1]], dsts=[T.land[:, rank:rank + 1]]) for j, mask in call],
+            local_sem=sem.sent)
+        sent[0] += sum(pop(tr[1]) for tr in call)
+
+    def bcast(w):
+        for call in bcast_calls(rank, w):
+            g.remote_dma_fused(
+                [RemoteDMATransfer(dst_ids=[dst_id(j) for j in dsts], dma_engine_mask=mask, remote_sem=sem[name],
+                                   srcs=[T.d[i]], dsts=[T.d[i] for j in dsts]) for i, dsts, mask, name in call],
+                local_sem=sem.sent)
+            sent[0] += sum(pop(tr[2]) for tr in call)
+
+    rows = 128 // WAVES
+    per = PIECES // WAVES
+    calls1 = a2a_calls(rank)
+
+    if rank == 8:
+        for w in range(WAVES):
+            q = g.sync if w == 0 else g.scalar
+            q.dma_start(T.d[w * per:(w + 1) * per], T.x2[w * rows:(w + 1) * rows, :]).then_inc(sem["ld2%d" % w], 16)
+
+    g.scalar.dma_start(T.s1[:], T.x1[:]).then_inc(sem.ld1, 16)
+    g.scalar.wait_ge(sem.ld1, 16)
+    g.scalar.dma_start(T.land[:, rank:rank + 1], T.s1[:, rank:rank + 1]).then_inc(sem.arr1, 16)
+    g.scalar.wait_ge(sem.arr1, exp["arr1"] + 16)
+    g.scalar.dma_start(T.y1[:], T.land[:]).then_inc(sem.st1, 16)
+
+    if rank == 8:
+        for w in range(WAVES):
+            g.wait_ge(sem["ld2%d" % w], 16)
+            bcast(w)
+        g.wait_ge(sem.ld1, 16)
+        for call in calls1:
+            a2a(call)
+        g.sem_inc(sem.go, 1)
+        g.sync.wait_ge(sem.go, 1)
+        g.sync.dma_start(T.y2[:], T.x2[:]).then_inc(sem.st2, 16)
+        g.wait_ge(sem.st2, 16)
+    else:
+        g.wait_ge(sem.ld1, 16)
+        a2a(calls1[0])
+        for w in range(WAVES):
+            g.wait_ge(sem["own%d" % w], exp["own%d" % w])
+            bcast(w)
+        for call in calls1[1:]:
+            a2a(call)
+        for w in range(WAVES):
+            g.sync.wait_ge(sem["own%d" % w], exp["own%d" % w])
+            g.sync.wait_ge(sem["arr2%d" % w], exp["arr2%d" % w])
+            g.sync.dma_start(T.y2[w * rows:(w + 1) * rows, :], T.d[w * per:(w + 1) * per]).then_inc(sem.st2, 16)
+        g.wait_ge(sem.st2, 16 * WAVES)
+    g.wait_ge(sem.st1, 16)
+    g.wait_ge(sem.sent, sent[0])

@@ -1,6 +1,6 @@
 from concourse.bass import DstId, RemoteDMATransfer
 
-WAVES = 1
+WAVES = 2
 SPLIT = True
 ROOT_CARRIES = False
 DUP_A = False

@@ -2,14 +2,13 @@ from concourse.bass import DstId, RemoteDMATransfer
 
 WAVES = 2
 SPLIT = True
-ROOT_CARRIES = False
 DUP_A = False
 
-PIECES = 16
+PIECES = 8 * WAVES
 SCRATCH = {
     "s1": ("sbuf", [128, 16], "float32"),
     "land": ("sbuf", [128, 16], "float32"),
-    "d": ("dram", [PIECES, 128, 32], "float32"),
+    "d": ("dram", [PIECES, 128, 512 // PIECES], "float32"),
 }
 SEMAPHORES = ["ld1", "arr1", "st1", "sent", "go", "st2"] + [n + str(w) for w in range(WAVES) for n in ("ld2", "own", "arr2")]
 
@@ -26,51 +25,33 @@ def a2a_calls(r):
     near = [j for j in range(16) if j // 8 == r // 8 and j != r]
     far = [j for j in range(16) if j // 8 != r // 8]
     on = [(j, bits(8 + i, 1)) for i, j in enumerate(near)]
-    if SPLIT and r > 8 and not ROOT_CARRIES:
+    if SPLIT and r > 8:
         return [on + [(j, bits(2 * i, 2)) for i, j in enumerate(far[:4])],
                 [(j, bits(2 * i, 2)) for i, j in enumerate(far[4:])]]
     return [on + [(j, bits(i, 1)) for i, j in enumerate(far)]]
 
 
-def wave(w):
-    n = PIECES // WAVES
-    return list(range(w * n, (w + 1) * n))
+def a_owners(m):
+    return [m % 4, 4 + m % 4] if DUP_A else [m]
 
 
-def carrier(i):
-    return 1 if i % 8 < 2 else i % 8
-
-
-def a_owners(i):
-    return [i % 4, 4 + i % 4] if DUP_A else [i % 8]
-
-
-def bcast_calls(rank, w):
+def bcast_call(rank, w):
     own, arr = "own%d" % w, "arr2%d" % w
     if rank == 8:
-        ps = wave(w)
-        if ROOT_CARRIES:
-            calls = []
-            for c in range(0, len(ps), 8):
-                part = ps[c:c + 8]
-                calls.append([(i, a_owners(i), bits(t, 1), own) for t, i in enumerate(part)]
-                             + [(i, [8 + carrier(i)], bits(8 + t, 1), own) for t, i in enumerate(part)])
-            return calls
-        e = 16 // len(ps)
-        return [[(i, [8 + carrier(i)], bits(t * e, e), own) for t, i in enumerate(ps)]]
+        return [(8 * w + m, a_owners(0) if m == 0 else [8 + m], bits(2 * m, 2), own) for m in range(8)]
     if rank > 8:
-        ps = [i for i in wave(w) if carrier(i) == rank - 8]
+        i = 8 * w + rank - 8
         others = [j for j in range(9, 16) if j != rank]
-        if ROOT_CARRIES:
-            e = 16 // len(ps)
-            return [[(i, others, bits(t * e, e), arr) for t, i in enumerate(ps)]]
-        e = 8 // len(ps)
-        return [[(i, a_owners(i), bits(t * e, e), own) for t, i in enumerate(ps)]
-                + [(i, others, bits(8 + t * e, e), arr) for t, i in enumerate(ps)]]
-    ps = [i for i in wave(w) if rank in a_owners(i)]
-    e = 16 // len(ps)
+        return [(i, a_owners(rank - 8), bits(0, 4), own), (i, others[:2], bits(4, 4), arr), (i, others[2:], bits(8, 8), arr)]
+    ms = [m for m in range(8) if rank in a_owners(m)]
+    e = 16 // len(ms)
     mates = [j for j in range(8) if j != rank and (j // 4 == rank // 4 or not DUP_A)]
-    return [[(i, mates, bits(t * e, e), arr) for t, i in enumerate(ps)]]
+    return [(8 * w + m, mates, bits(t * e, e), arr) for t, m in enumerate(ms)]
+
+
+def root_spread():
+    e = 16 // WAVES
+    return [(8 * w, list(range(9, 16)), bits(w * e, e), "arr2%d" % w) for w in range(WAVES)]
 
 
 def expect(rank):
@@ -80,11 +61,10 @@ def expect(rank):
             for j, mask in call:
                 if j == rank:
                     n["arr1"] = n.get("arr1", 0) + pop(mask)
-        for w in range(WAVES):
-            for call in bcast_calls(s, w):
-                for tr in call:
-                    if rank in tr[1]:
-                        n[tr[3]] = n.get(tr[3], 0) + pop(tr[2])
+        for call in [bcast_call(s, w) for w in range(WAVES)] + ([root_spread()] if s == 8 else []):
+            for tr in call:
+                if rank in tr[1]:
+                    n[tr[3]] = n.get(tr[3], 0) + pop(tr[2])
     return n
 
 
@@ -107,22 +87,20 @@ def rank_program(g, core, T, topo):
             local_sem=sem.sent)
         sent[0] += sum(pop(tr[1]) for tr in call)
 
-    def bcast(w):
-        for call in bcast_calls(rank, w):
-            g.remote_dma_fused(
-                [RemoteDMATransfer(dst_ids=[dst_id(j) for j in dsts], dma_engine_mask=mask, remote_sem=sem[name],
-                                   srcs=[T.d[i]], dsts=[T.d[i] for j in dsts]) for i, dsts, mask, name in call],
-                local_sem=sem.sent)
-            sent[0] += sum(pop(tr[2]) for tr in call)
+    def bcast(call):
+        g.remote_dma_fused(
+            [RemoteDMATransfer(dst_ids=[dst_id(j) for j in dsts], dma_engine_mask=mask, remote_sem=sem[name],
+                               srcs=[T.d[i]], dsts=[T.d[i] for j in dsts]) for i, dsts, mask, name in call],
+            local_sem=sem.sent)
+        sent[0] += sum(pop(tr[2]) for tr in call)
 
     rows = 128 // WAVES
-    per = PIECES // WAVES
     calls1 = a2a_calls(rank)
 
     if rank == 8:
         for w in range(WAVES):
-            q = g.sync if w == 0 else g.scalar
-            q.dma_start(T.d[w * per:(w + 1) * per], T.x2[w * rows:(w + 1) * rows, :]).then_inc(sem["ld2%d" % w], 16)
+            q = g.sync if w % 2 == 0 else g.scalar
+            q.dma_start(T.d[w * 8:(w + 1) * 8], T.x2[w * rows:(w + 1) * rows, :]).then_inc(sem["ld2%d" % w], 16)
 
     g.scalar.dma_start(T.s1[:], T.x1[:]).then_inc(sem.ld1, 16)
     g.scalar.wait_ge(sem.ld1, 16)
@@ -133,7 +111,8 @@ def rank_program(g, core, T, topo):
     if rank == 8:
         for w in range(WAVES):
             g.wait_ge(sem["ld2%d" % w], 16)
-            bcast(w)
+            bcast(bcast_call(rank, w))
+        bcast(root_spread())
         g.wait_ge(sem.ld1, 16)
         for call in calls1:
             a2a(call)
@@ -146,13 +125,13 @@ def rank_program(g, core, T, topo):
         a2a(calls1[0])
         for w in range(WAVES):
             g.wait_ge(sem["own%d" % w], exp["own%d" % w])
-            bcast(w)
+            bcast(bcast_call(rank, w))
         for call in calls1[1:]:
             a2a(call)
         for w in range(WAVES):
             g.sync.wait_ge(sem["own%d" % w], exp["own%d" % w])
             g.sync.wait_ge(sem["arr2%d" % w], exp["arr2%d" % w])
-            g.sync.dma_start(T.y2[w * rows:(w + 1) * rows, :], T.d[w * per:(w + 1) * per]).then_inc(sem.st2, 16)
+            g.sync.dma_start(T.y2[w * rows:(w + 1) * rows, :], T.d[w * 8:(w + 1) * 8]).then_inc(sem.st2, 16)
         g.wait_ge(sem.st2, 16 * WAVES)
     g.wait_ge(sem.st1, 16)
     g.wait_ge(sem.sent, sent[0])

from concourse.bass import DstId, RemoteDMATransfer

WAVES = 2
SPLIT = True
DUP_A = False

PIECES = 8 * WAVES
SCRATCH = {
    "s1": ("sbuf", [128, 16], "float32"),
    "land": ("sbuf", [128, 16], "float32"),
    "d": ("dram", [PIECES, 128, 512 // PIECES], "float32"),
}
SEMAPHORES = ["ld1", "arr1", "st1", "sent", "go", "st2"] + [n + str(w) for w in range(WAVES) for n in ("ld2", "own", "arr2")]


def bits(lo, n):
    return ((1 << n) - 1) << lo


def pop(mask):
    return bin(mask).count("1")


def a2a_calls(r):
    near = [j for j in range(16) if j // 8 == r // 8 and j != r]
    far = [j for j in range(16) if j // 8 != r // 8]
    on = [(j, bits(8 + i, 1)) for i, j in enumerate(near)]
    if SPLIT and r > 8:
        return [on + [(j, bits(2 * i, 2)) for i, j in enumerate(far[:4])],
                [(j, bits(2 * i, 2)) for i, j in enumerate(far[4:])]]
    return [on + [(j, bits(i, 1)) for i, j in enumerate(far)]]


def a_owners(m):
    return [m % 4, 4 + m % 4] if DUP_A else [m]


def bcast_call(rank, w):
    own, arr = "own%d" % w, "arr2%d" % w
    if rank == 8:
        return [(8 * w + m, a_owners(0) if m == 0 else [8 + m], bits(2 * m, 2), own) for m in range(8)]
    if rank > 8:
        i = 8 * w + rank - 8
        others = [j for j in range(9, 16) if j != rank]
        return [(i, a_owners(rank - 8), bits(0, 4), own), (i, others[:2], bits(4, 4), arr), (i, others[2:], bits(8, 8), arr)]
    ms = [m for m in range(8) if rank in a_owners(m)]
    e = 16 // len(ms)
    mates = [j for j in range(8) if j != rank and (j // 4 == rank // 4 or not DUP_A)]
    return [(8 * w + m, mates, bits(t * e, e), arr) for t, m in enumerate(ms)]


def root_spread():
    e = 16 // WAVES
    return [(8 * w, list(range(9, 16)), bits(w * e, e), "arr2%d" % w) for w in range(WAVES)]


def expect(rank):
    n = {}
    for s in range(16):
        for call in a2a_calls(s):
            for j, mask in call:
                if j == rank:
                    n["arr1"] = n.get("arr1", 0) + pop(mask)
        for call in [bcast_call(s, w) for w in range(WAVES)] + ([root_spread()] if s == 8 else []):
            for tr in call:
                if rank in tr[1]:
                    n[tr[3]] = n.get(tr[3], 0) + pop(tr[2])
    return n


def rank_program(g, core, T, topo):
    rank = T.rank_of(core)
    if rank is None:
        return
    sem = T.sem
    exp = expect(rank)
    sent = [0]

    def dst_id(j):
        rid, pid = topo.addr(T.cores[j], core)
        return DstId(rid=rid, pnc=pid)

    def a2a(call):
        g.remote_dma_fused(
            [RemoteDMATransfer(dst_ids=[dst_id(j)], dma_engine_mask=mask, remote_sem=sem.arr1,
                               srcs=[T.s1[:, j:j + 1]], dsts=[T.land[:, rank:rank + 1]]) for j, mask in call],
            local_sem=sem.sent)
        sent[0] += sum(pop(tr[1]) for tr in call)

    def bcast(call):
        g.remote_dma_fused(
            [RemoteDMATransfer(dst_ids=[dst_id(j) for j in dsts], dma_engine_mask=mask, remote_sem=sem[name],
                               srcs=[T.d[i]], dsts=[T.d[i] for j in dsts]) for i, dsts, mask, name in call],
            local_sem=sem.sent)
        sent[0] += sum(pop(tr[2]) for tr in call)

    rows = 128 // WAVES
    calls1 = a2a_calls(rank)

    if rank == 8:
        for w in range(WAVES):
            q = g.sync if w % 2 == 0 else g.scalar
            q.dma_start(T.d[w * 8:(w + 1) * 8], T.x2[w * rows:(w + 1) * rows, :]).then_inc(sem["ld2%d" % w], 16)

    g.scalar.dma_start(T.s1[:], T.x1[:]).then_inc(sem.ld1, 16)
    g.scalar.wait_ge(sem.ld1, 16)
    g.scalar.dma_start(T.land[:, rank:rank + 1], T.s1[:, rank:rank + 1]).then_inc(sem.arr1, 16)
    g.scalar.wait_ge(sem.arr1, exp["arr1"] + 16)
    g.scalar.dma_start(T.y1[:], T.land[:]).then_inc(sem.st1, 16)

    if rank == 8:
        for w in range(WAVES):
            g.wait_ge(sem["ld2%d" % w], 16)
            bcast(bcast_call(rank, w))
        bcast(root_spread())
        g.wait_ge(sem.ld1, 16)
        for call in calls1:
            a2a(call)
        g.sem_inc(sem.go, 1)
        g.sync.wait_ge(sem.go, 1)
        g.sync.dma_start(T.y2[:], T.x2[:]).then_inc(sem.st2, 16)
        g.wait_ge(sem.st2, 16)
    else:
        g.wait_ge(sem.ld1, 16)
        a2a(calls1[0])
        for w in range(WAVES):
            g.wait_ge(sem["own%d" % w], exp["own%d" % w])
            bcast(bcast_call(rank, w))
        for call in calls1[1:]:
            a2a(call)
        for w in range(WAVES):
            g.sync.wait_ge(sem["own%d" % w], exp["own%d" % w])
            g.sync.wait_ge(sem["arr2%d" % w], exp["arr2%d" % w])
            g.sync.dma_start(T.y2[w * rows:(w + 1) * rows, :], T.d[w * 8:(w + 1) * 8]).then_inc(sem.st2, 16)
        g.wait_ge(sem.st2, 16 * WAVES)
    g.wait_ge(sem.st1, 16)
    g.wait_ge(sem.sent, sent[0])
